import numpy as np
import ml_dtypes


def mxq(x, axis, fmt="e4m3"):
    dtype, down = {"e4m3": (ml_dtypes.float8_e4m3fn, 7), "e5m2": (ml_dtypes.float8_e5m2, 14)}[fmt]
    v = np.moveaxis(np.asarray(x, np.float32).astype(ml_dtypes.bfloat16).astype(np.float64), axis, -1)
    blocks = v.reshape(v.shape[:-1] + (-1, 32))
    amax = np.abs(blocks).max(-1, keepdims=True)
    byte = np.maximum(np.where(amax > 0, np.frexp(amax)[1] - 1 + 127, 0) - down, 1)
    scale = np.exp2(byte - 127.0)
    codes = (blocks / scale).astype(np.float32).astype(dtype).astype(np.float64)
    return np.moveaxis((codes * scale).reshape(v.shape), -1, axis)


WIDE = False


def mx_kscale(k):
    if not WIDE:
        return np.ones(k)
    levels = np.array([10, -10, 5, -5, 0])
    if k % 512:
        return np.exp2(np.random.permutation(np.resize(levels, k // 32))).repeat(32)
    a = np.empty((k // 512, 16))
    for p in range(k // 512):
        a[p, :8] = np.random.permutation(np.resize(levels, 8))
        for g in range(8):
            far = levels[np.abs(levels - a[p, g]) >= 10]
            a[p, g + 8] = far[np.random.randint(len(far))]
    return np.exp2(a.ravel()).repeat(32)


def f64(x):
    return np.asarray(x).astype(np.float64)


def striped(idx):
    return np.tile(np.asarray(idx).reshape(-1, 16).T, (8, 1)).astype(np.uint16)


def unstriped(offs):
    return offs[:16].T.reshape(-1).astype(np.int64)


E2M1 = np.array([0.0, 0.5, 1.0, 1.5, 2.0, 3.0, 4.0, 6.0, -0.0, -0.5, -1.0, -1.5, -2.0, -3.0, -4.0, -6.0])


def pack_weight(w, fmt):
    k, n = w.shape
    w = f64(np.asarray(w, np.float32).astype(ml_dtypes.bfloat16)).reshape(k // 32, 32, n)
    amax = np.abs(w).max(1)
    if fmt == "e4m3":
        byte = np.frexp(amax)[1] - 1 + 127 - 7
    else:
        mant, ex = np.frexp(amax / 6.0)
        byte = np.where(mant > 0.5, ex, ex - 1) + 127
    byte = np.clip(np.where(amax > 0, byte, 1), 1, 254)
    scaled = (w * np.exp2(127.0 - byte)[:, None, :]).reshape(k, n).astype(np.float32)
    by_word = np.ascontiguousarray(scaled.reshape(k // 512, 128, 4, n).transpose(0, 1, 3, 2))
    if fmt == "e4m3":
        words = by_word.astype(ml_dtypes.float8_e4m3fn).view(np.uint8)
    else:
        c = by_word.astype(ml_dtypes.float4_e2m1fn).view(np.uint8) & 0xF
        words = (c[..., 0::2] | (c[..., 1::2] << 4)).reshape(k // 512, 128, 2 * n)
    return np.ascontiguousarray(words), np.ascontiguousarray(byte.astype(np.uint8).reshape(k // 512, 16, n))


def unpack_weight(words, scales, fmt):
    g, _, n = scales.shape
    words = np.ascontiguousarray(words).reshape(g, 128, n, -1)
    if fmt == "e4m3":
        vals = words.view(ml_dtypes.float8_e4m3fn).astype(np.float64)
    else:
        nib = np.empty((g, 128, n, 4), np.uint8)
        nib[..., 0::2] = words & 0xF
        nib[..., 1::2] = words >> 4
        vals = E2M1[nib]
    vals = vals * np.repeat(np.exp2(scales.astype(np.float64) - 127.0), 8, axis=1)[..., None]
    return vals.transpose(0, 1, 3, 2).reshape(g * 512, n)


D, T, I, Q, E, J, C = 512, 2048, 512, 128, 512, 512, 1024


def setup_inputs():
    n = np.random.standard_normal
    idx = np.random.permutation(T)[:I]
    fd = mx_kscale(D)
    fc = mx_kscale(C)
    keysp = pack_weight(n((D, T)) / fd[:, None], "e4m3")
    return {
        "query": (n((D, Q)) * 0.4 / np.sqrt(D) * fd[:, None]).astype(np.float32),
        "keys_words": keysp[0],
        "keys_scales": keysp[1],
        "dkey": (n((D, J)) / fd[:, None]).astype(np.float32),
        "mask": (np.where(np.random.uniform(size=(Q, J)) < 0.3, 0.0, -30.0)).astype(np.float32),
        "fac": (np.random.uniform(0.5, 2.0, (1, C)) * fc).astype(np.float32),
        "vals": (n((C, E)) / fc[:, None]).astype(np.float32),
        "offs": striped(idx),
    }


def reference(query, keys_words, keys_scales, dkey, mask, fac, vals, offs):
    idx = unstriped(offs)
    keysu = unpack_weight(keys_words, keys_scales, "e4m3")
    queryq = mxq(f64(query), 0, "e4m3")
    keysidxg = keysu[:, idx]
    a = queryq.T @ keysidxg
    dkeyq = mxq(f64(dkey), 0, "e4m3")
    b = queryq.T @ dkeyq
    bm = b + f64(mask)
    s = np.concatenate([a, bm], axis=1)
    p = np.exp(s - np.max(s, axis=1, keepdims=True))
    w = p * f64(fac) / np.sum(p, axis=1, keepdims=True)
    wt = w.T
    wtq = mxq(wt, 0, "e4m3")
    valsq = mxq(f64(vals), 0, "e4m3")
    o = wtq.T @ valsq
    return o

@@ -1,0 +1,202 @@
+from contextlib import ExitStack
+
+import concourse.mybir as mybir
+from concourse.masks import make_identity
+
+D, T, I, Q, E, J, C = 512, 2048, 512, 128, 512, 512, 1024
+FLOPS = 2 * Q * D * (I + J) + 2 * Q * C * E
+
+F32 = mybir.dt.float32
+BF16 = mybir.dt.bfloat16
+I32 = mybir.dt.int32
+U32 = mybir.dt.uint32
+U16 = mybir.dt.uint16
+U8 = mybir.dt.uint8
+FP8X4 = mybir.dt.float8_e4m3fn_x4
+ALU = mybir.AluOpType
+ACT = mybir.ActivationFunctionType
+AX = mybir.AxisListType
+
+P = 128
+HALF = 256
+PIECE = 128
+
+
+def interleave(copy, grouped, raw, c0, width):
+    copy(
+        grouped[:, c0 : c0 + width, :].rearrange("p (c i) t -> p c t i", i=4),
+        raw[:, :, c0 : c0 + width].rearrange("p t (c i) -> p c t i", i=4),
+    )
+
+
+def tile_attend_treeverify_kernel(tc, query, keys_words, keys_scales, dkey, mask, fac, vals, offs, out):
+    nc = tc.nc
+    with ExitStack() as ctx:
+        sb = ctx.enter_context(tc.tile_pool(name="sb", bufs=1))
+        ps = ctx.enter_context(tc.psum_pool(name="ps", bufs=1))
+
+        def operand(name, width):
+            raw = sb.tile([P, 4, width], F32, name=name + "_raw", align_bytes=64)
+            grouped = sb.tile([P, width, 4], BF16, name=name + "_grouped", align_bytes=64)
+            codes = sb.tile([P, width], U32, name=name + "_codes", align_bytes=64)
+            scales = sb.tile([P, width], U8, name=name + "_scales", align_bytes=64)
+            return raw, grouped, codes, scales
+
+        def quantize(codes, scales, grouped):
+            nc.vector.quantize_mx(
+                out=codes[:].bitcast(FP8X4), scales=scales[:], in_=grouped[:].rearrange("p w t -> p (w t)")
+            )
+
+        def product(acc, lhs_codes, lhs_scales, rhs_codes, rhs_scales, start, stop):
+            nc.tensor.matmul_mx(
+                out=acc,
+                lhsT=lhs_codes.bitcast(FP8X4),
+                lhsT_scale=lhs_scales,
+                rhs=rhs_codes.bitcast(FP8X4),
+                rhs_scale=rhs_scales,
+                start=start,
+                stop=stop,
+            )
+
+        offsets = sb.tile([P, I // 16], U16, name="offsets")
+        pool_scales = sb.tile([P, T], U8, name="pool_scales", align_bytes=64)
+        pool_words = sb.tile([P, T], I32, name="pool_words", align_bytes=64)
+        mask_sb = sb.tile([P, J], F32, name="mask_sb", align_bytes=64)
+        fac_cols = sb.tile([P, 2, 4], F32, name="fac_cols", align_bytes=64)
+        q_op = operand("q", Q)
+        d_op = [operand("d%d" % h, HALF) for h in range(2)]
+        v_order = [(1, 0), (0, 0), (1, 1), (0, 1)]
+        v_op = {gh: operand("v%d%d" % gh, HALF) for gh in v_order}
+
+        nc.vector.memset(pool_scales[:].bitcast(I32), 0)
+        nc.sync.dma_start(offsets[:], offs)
+        nc.sync.dma_start(q_op[0][:], query.rearrange("(p t) w -> p t w", t=4))
+        dkey_rows = dkey.rearrange("(p t) w -> p t w", t=4)
+        nc.sync.dma_start(d_op[0][0][:], dkey_rows[:, :, 0:HALF])
+        for quad in range(4):
+            nc.scalar.dma_start(
+                pool_scales[32 * quad : 32 * quad + 4, :].bitcast(I32),
+                keys_scales[0, 4 * quad : 4 * quad + 4, :].bitcast(I32),
+            )
+        nc.sync.dma_start(d_op[1][0][:], dkey_rows[:, :, HALF:J])
+        nc.sync.dma_start(mask_sb[:], mask)
+        nc.sync.dma_start(pool_words[:], keys_words[0].rearrange("p n t -> p (n t)").bitcast(I32))
+        nc.sync.dma_start(fac_cols[:], fac.rearrange("o (g p t) -> p (o g) t", g=2, t=4))
+        val_rows = vals.rearrange("(g p t) w -> g p t w", g=2, t=4)
+        for g, h in v_order:
+            nc.sync.dma_start(v_op[g, h][0][:], val_rows[g][:, :, h * HALF : (h + 1) * HALF])
+
+        ident = sb.tile([P, P], F32, name="ident", align_bytes=64)
+        make_identity(nc, ident[:])
+        warm = sb.tile([P, 1], F32, name="warm")
+        nc.scalar.activation(warm[:], ident[:, 0:1], ACT.Exp)
+
+        interleave(nc.scalar.copy, q_op[1], q_op[0], 0, Q)
+        key_scales = sb.tile([P, I], U8, name="key_scales", align_bytes=64)
+        nc.vector.tensor_copy(key_scales[:], pool_scales[:].indirect(offsets[:]))
+        quantize(q_op[2], q_op[3], q_op[1])
+
+        bm = sb.tile([P, J], F32, name="bm", align_bytes=64)
+        b_ps = [ps.tile([P, HALF], F32, name="b_ps%d" % h, tag="bank%d" % h) for h in range(2)]
+        for h in range(2):
+            raw, grouped, codes, scales = d_op[h]
+            interleave(nc.scalar.copy, grouped, raw, 0, PIECE)
+            interleave(nc.vector.tensor_copy if h == 1 else nc.scalar.copy, grouped, raw, PIECE, PIECE)
+            quantize(codes, scales, grouped)
+            product(b_ps[h][:], q_op[2][:], q_op[3][:], codes[:], scales[:], True, True)
+        for h in range(2):
+            cols = slice(h * HALF, (h + 1) * HALF)
+            nc.vector.tensor_tensor(bm[:, cols], b_ps[h][:], mask_sb[:, cols], ALU.add)
+        neg_max_b = sb.tile([P, 1], F32, name="neg_max_b")
+        nc.vector.tensor_reduce(neg_max_b[:], bm[:], AX.X, ALU.max, negate=True)
+        p_b = sb.tile([P, 2, P, 2], F32, name="p_b", align_bytes=64)
+        sum_b = sb.tile([P, 1], F32, name="sum_b")
+        nc.scalar.activation(
+            p_b[:], bm[:].rearrange("q (p u e) -> q u p e", u=2, e=2), ACT.Exp, bias=neg_max_b[:], accum_out=sum_b[:]
+        )
+
+        neg_a = sb.tile([P, 2, P, 2], F32, name="neg_a", align_bytes=64)
+        key_words = [sb.tile([P, HALF], U32, name="key_words%d" % h, align_bytes=64) for h in range(2)]
+        a_ps = [ps.tile([P, HALF], F32, name="a_ps%d" % h, tag="bank%d" % (2 + h)) for h in range(2)]
+        for h in range(2):
+            nc.vector.tensor_copy(
+                key_words[h][:], pool_words[:].bitcast(U32).indirect(offsets[:, 16 * h : 16 * (h + 1)])
+            )
+            product(
+                a_ps[h][:], q_op[2][:], q_op[3][:], key_words[h][:], key_scales[:, h * HALF : (h + 1) * HALF], True, True
+            )
+        neg_max = neg_max_b
+        for h in range(2):
+            lower = sb.tile([P, 1], F32, name="neg_max%d" % h)
+            nc.vector.tensor_scalar(
+                neg_a[:, :, 64 * h : 64 * (h + 1), :],
+                a_ps[h][:].rearrange("q (p u e) -> q u p e", u=2, e=2),
+                -1.0,
+                neg_max[:],
+                ALU.mult,
+                ALU.min,
+                accum_out=lower[:],
+            )
+            neg_max = lower
+
+        fac_ps = [ps.tile([P, 4, P], F32, name="fac_ps%d" % g, tag="bank%d" % (4 + g)) for g in range(2)]
+        for g in range(2):
+            for t in range(4):
+                nc.tensor.transpose(fac_ps[g][:, t, :], fac_cols[:, g, t : t + 1].to_broadcast([P, P]), ident[:])
+
+        shift_b = sb.tile([P, 1], F32, name="shift_b")
+        nc.scalar.activation(shift_b[:], neg_max_b[:], ACT.Exp, bias=neg_max[:], scale=-1.0)
+        p_a = sb.tile([P, 2, P, 2], F32, name="p_a", align_bytes=64)
+        sum_a = sb.tile([P, 1], F32, name="sum_a")
+        nc.scalar.activation(p_a[:], neg_a[:], ACT.Exp, bias=neg_max[:], scale=-1.0, accum_out=sum_a[:])
+
+        def fac_view(g, u):
+            return fac_ps[g][:, 2 * u : 2 * u + 2, :].rearrange("q e p -> q p e")
+
+        pf_b = sb.tile([P, 2, P, 2], F32, name="pf_b", align_bytes=64)
+        for u in range(2):
+            nc.vector.scalar_tensor_tensor(pf_b[:, u], p_b[:, u], shift_b[:], fac_view(1, u), ALU.mult, ALU.mult)
+        total = sb.tile([P, 1], F32, name="total")
+        nc.vector.tensor_scalar(total[:], sum_b[:], shift_b[:], sum_a[:], ALU.mult, ALU.add)
+        inv = sb.tile([P, 1], F32, name="inv")
+        nc.vector.reciprocal(inv[:], total[:])
+
+        w = {(g, u): sb.tile([P, P, 2], BF16, name="w%d%d" % (g, u), align_bytes=64) for g in range(2) for u in range(2)}
+        for u in range(2):
+            nc.vector.scalar_tensor_tensor(w[0, u][:], p_a[:, u], inv[:], fac_view(0, u), ALU.mult, ALU.mult)
+            nc.scalar.activation(w[1, u][:], pf_b[:, u], ACT.Copy, scale=inv[:])
+
+        wt_ps = [ps.tile([P, 2, P], F32, name="wt_ps%d" % g, tag="bank%d" % (6 + g)) for g in range(2)]
+        for u in range(2):
+            for g in range(2):
+                nc.tensor.transpose(
+                    wt_ps[g][:, u, :], w[g, u][:].rearrange("q p e -> q (p e)").bitcast(F32), ident[:]
+                )
+        w_codes, w_scales = [], []
+        for g in range(2):
+            grouped = sb.tile([P, Q, 4], BF16, name="wt_grouped%d" % g, align_bytes=64)
+            w_codes.append(sb.tile([P, Q], U32, name="wt_codes%d" % g, align_bytes=64))
+            w_scales.append(sb.tile([P, Q], U8, name="wt_scales%d" % g, align_bytes=64))
+            copy = nc.vector.tensor_copy if g == 0 else nc.scalar.copy
+            copy(
+                grouped[:].rearrange("p q t -> p (q t)").bitcast(F32).rearrange("p (q u) -> p q u", u=2),
+                wt_ps[g][:].rearrange("p u q -> p q u"),
+            )
+            quantize(w_codes[g], w_scales[g], grouped)
+
+        for n, gh in enumerate(v_order):
+            raw, grouped, codes, scales = v_op[gh]
+            interleave(nc.scalar.copy, grouped, raw, 0, PIECE)
+            interleave(nc.vector.tensor_copy if n >= 2 else nc.scalar.copy, grouped, raw, PIECE, PIECE)
+            quantize(codes, scales, grouped)
+
+        for h in range(2):
+            acc = ps.tile([P, HALF], F32, name="o_ps%d" % h, tag="bank%d" % h)
+            for g in (1, 0):
+                product(acc[:], w_codes[g][:], w_scales[g][:], v_op[g, h][2][:], v_op[g, h][3][:], g == 1, g == 0)
+            result = sb.tile([P, HALF], F32, name="result%d" % h, align_bytes=64)
+            if h == 0:
+                nc.scalar.copy(result[:], acc[:])
+            else:
+                nc.vector.tensor_copy(result[:], acc[:])
+            nc.sync.dma_start(out[:, h * HALF : (h + 1) * HALF], result[:])

@@ -20,11 +20,12 @@ AX = mybir.AxisListType
 P = 128
 HALF = 256
 PIECE = 128
+SCALAR_SHARE = 96
 
 
-def interleave(copy, grouped, raw, c0, width):
+def interleave(copy, grouped, raw, g0, c0, width):
     copy(
-        grouped[:, c0 : c0 + width, :].rearrange("p (c i) t -> p c t i", i=4),
+        grouped[:, g0 : g0 + width, :].rearrange("p (c i) t -> p c t i", i=4),
         raw[:, :, c0 : c0 + width].rearrange("p t (c i) -> p c t i", i=4),
     )
 
@@ -35,17 +36,20 @@ def tile_attend_treeverify_kernel(tc, query, keys_words, keys_scales, dkey, mask
         sb = ctx.enter_context(tc.tile_pool(name="sb", bufs=1))
         ps = ctx.enter_context(tc.psum_pool(name="ps", bufs=1))
 
-        def operand(name, width):
-            raw = sb.tile([P, 4, width], F32, name=name + "_raw", align_bytes=64)
-            grouped = sb.tile([P, width, 4], BF16, name=name + "_grouped", align_bytes=64)
-            codes = sb.tile([P, width], U32, name=name + "_codes", align_bytes=64)
-            scales = sb.tile([P, width], U8, name=name + "_scales", align_bytes=64)
-            return raw, grouped, codes, scales
+        def raw_tile(name, width):
+            return sb.tile([P, 4, width], F32, name=name + "_raw", tag=name + "_raw", align_bytes=64)
 
-        def quantize(codes, scales, grouped):
+        def grouped_tile(name, width, tag=None):
+            return sb.tile([P, width, 4], BF16, name=name + "_grouped", tag=tag or name + "_grouped", align_bytes=64)
+
+        def quantize(name, grouped, tag=None):
+            width = grouped.shape[1]
+            codes = sb.tile([P, width], U32, name=name + "_codes", tag=tag or name + "_codes", align_bytes=64)
+            scales = sb.tile([P, width], U8, name=name + "_scales", align_bytes=64)
             nc.vector.quantize_mx(
                 out=codes[:].bitcast(FP8X4), scales=scales[:], in_=grouped[:].rearrange("p w t -> p (w t)")
             )
+            return codes, scales
 
         def product(acc, lhs_codes, lhs_scales, rhs_codes, rhs_scales, start, stop):
             nc.tensor.matmul_mx(
@@ -61,142 +65,154 @@ def tile_attend_treeverify_kernel(tc, query, keys_words, keys_scales, dkey, mask
         offsets = sb.tile([P, I // 16], U16, name="offsets")
         pool_scales = sb.tile([P, T], U8, name="pool_scales", align_bytes=64)
         pool_words = sb.tile([P, T], I32, name="pool_words", align_bytes=64)
-        mask_sb = sb.tile([P, J], F32, name="mask_sb", align_bytes=64)
+        mask_sb = sb.tile([P, J], F32, name="mask_sb", tag="mask_sb", align_bytes=64)
         fac_cols = sb.tile([P, 2, 4], F32, name="fac_cols", align_bytes=64)
-        q_op = operand("q", Q)
-        d_op = [operand("d%d" % h, HALF) for h in range(2)]
-        v_order = [(1, 0), (0, 0), (1, 1), (0, 1)]
-        v_op = {gh: operand("v%d%d" % gh, HALF) for gh in v_order}
+        q_raw = raw_tile("q", Q)
+        d_raw = raw_tile("d", J)
+        v_raw = [raw_tile("v%d" % n, HALF) for n in range(4)]
+        val_rows = vals.rearrange("(g p t) w -> g p t w", g=2, t=4)
+
+        def load_values(n):
+            nc.sync.dma_start(v_raw[n][:], val_rows[1 - n // 2][:, :, (n % 2) * HALF : (n % 2 + 1) * HALF])
 
         nc.vector.memset(pool_scales[:].bitcast(I32), 0)
+        nc.scalar.dma_start(fac_cols[:], fac.rearrange("o (g p t) -> p (o g) t", g=2, t=4))
         nc.sync.dma_start(offsets[:], offs)
-        nc.sync.dma_start(q_op[0][:], query.rearrange("(p t) w -> p t w", t=4))
-        dkey_rows = dkey.rearrange("(p t) w -> p t w", t=4)
-        nc.sync.dma_start(d_op[0][0][:], dkey_rows[:, :, 0:HALF])
-        for quad in range(4):
-            nc.scalar.dma_start(
-                pool_scales[32 * quad : 32 * quad + 4, :].bitcast(I32),
-                keys_scales[0, 4 * quad : 4 * quad + 4, :].bitcast(I32),
-            )
-        nc.sync.dma_start(d_op[1][0][:], dkey_rows[:, :, HALF:J])
-        nc.sync.dma_start(mask_sb[:], mask)
         nc.sync.dma_start(pool_words[:], keys_words[0].rearrange("p n t -> p (n t)").bitcast(I32))
-        nc.sync.dma_start(fac_cols[:], fac.rearrange("o (g p t) -> p (o g) t", g=2, t=4))
-        val_rows = vals.rearrange("(g p t) w -> g p t w", g=2, t=4)
-        for g, h in v_order:
-            nc.sync.dma_start(v_op[g, h][0][:], val_rows[g][:, :, h * HALF : (h + 1) * HALF])
+        for r in range(4):
+            nc.sync.dma_start(pool_scales[r:P:32, :].bitcast(I32), keys_scales[0, r:16:4, :].bitcast(I32))
+        nc.sync.dma_start(q_raw[:], query.rearrange("(p t) w -> p t w", t=4))
+        nc.sync.dma_start(d_raw[:], dkey.rearrange("(p t) w -> p t w", t=4))
+        load_values(0)
+        nc.sync.dma_start(mask_sb[:], mask)
+        for n in range(1, 4):
+            load_values(n)
 
         ident = sb.tile([P, P], F32, name="ident", align_bytes=64)
         make_identity(nc, ident[:])
-        warm = sb.tile([P, 1], F32, name="warm")
-        nc.scalar.activation(warm[:], ident[:, 0:1], ACT.Exp)
 
-        interleave(nc.scalar.copy, q_op[1], q_op[0], 0, Q)
+        def spread(out_ap, g, t):
+            nc.tensor.transpose(out_ap, fac_cols[:, g, t : t + 1].to_broadcast([P, P]), ident[:])
+
+        fac_a_ps = ps.tile([P, 4, P], F32, name="fac_a_ps", tag="prefix_bank")
+        draft_banks = [ps.tile([P, 4, P], F32, name="draft_bank%d" % h) for h in range(2)]
+        for t in range(4):
+            spread(fac_a_ps[:, t, :], 0, t)
+        for t in range(4):
+            spread(draft_banks[t // 2][:, t % 2, :], 1, t)
+
+        def scalar_cast(out_ap, in_ap):
+            nc.scalar.activation(out_ap, in_ap, ACT.Copy)
+
+        fac_a = sb.tile([P, 2, P, 2], F32, name="fac_a", align_bytes=64)
+        scalar_cast(fac_a[:], fac_a_ps[:].rearrange("q (u e) p -> q u p e", u=2))
+
+        key_words = sb.tile([P, I], U32, name="key_words", align_bytes=64)
+        nc.vector.tensor_copy(key_words[:], pool_words[:].bitcast(U32).indirect(offsets[:]))
         key_scales = sb.tile([P, I], U8, name="key_scales", align_bytes=64)
         nc.vector.tensor_copy(key_scales[:], pool_scales[:].indirect(offsets[:]))
-        quantize(q_op[2], q_op[3], q_op[1])
+        q_grouped = grouped_tile("q", Q)
+        interleave(scalar_cast, q_grouped, q_raw, 0, 0, Q)
+        q_codes, q_scales = quantize("q", q_grouped)
+        a_ps = ps.tile([P, I], F32, name="a_ps", tag="prefix_bank")
+        product(a_ps[:], q_codes[:], q_scales[:], key_words[:], key_scales[:], True, True)
 
-        bm = sb.tile([P, J], F32, name="bm", align_bytes=64)
-        b_ps = [ps.tile([P, HALF], F32, name="b_ps%d" % h, tag="bank%d" % h) for h in range(2)]
+        d_grouped = [grouped_tile("d%d" % h, HALF) for h in range(2)]
         for h in range(2):
-            raw, grouped, codes, scales = d_op[h]
-            interleave(nc.scalar.copy, grouped, raw, 0, PIECE)
-            interleave(nc.vector.tensor_copy if h == 1 else nc.scalar.copy, grouped, raw, PIECE, PIECE)
-            quantize(codes, scales, grouped)
-            product(b_ps[h][:], q_op[2][:], q_op[3][:], codes[:], scales[:], True, True)
+            interleave(scalar_cast, d_grouped[h], d_raw, 0, h * HALF, SCALAR_SHARE)
+            interleave(nc.vector.tensor_copy, d_grouped[h], d_raw, SCALAR_SHARE, h * HALF + SCALAR_SHARE, HALF - SCALAR_SHARE)
+        b_ps = [bank[:, 2:4, :].rearrange("q a b -> q (a b)") for bank in draft_banks]
+        for h in range(2):
+            codes, scales = quantize("d%d" % h, d_grouped[h])
+            product(b_ps[h], q_codes[:], q_scales[:], codes[:], scales[:], True, True)
+
+        neg_a = sb.tile([P, 2, P, 2], F32, name="neg_a", tag="d0_grouped", align_bytes=64)
+        neg_max_a = sb.tile([P, 1], F32, name="neg_max_a")
+        nc.vector.tensor_scalar(
+            neg_a[:], a_ps[:].rearrange("q (p u e) -> q u p e", u=2, e=2), -1.0, None, ALU.mult, ALU.min,
+            accum_out=neg_max_a[:],
+        )
+        bm = sb.tile([P, J], F32, name="bm", tag="bm", align_bytes=64)
         for h in range(2):
             cols = slice(h * HALF, (h + 1) * HALF)
-            nc.vector.tensor_tensor(bm[:, cols], b_ps[h][:], mask_sb[:, cols], ALU.add)
-        neg_max_b = sb.tile([P, 1], F32, name="neg_max_b")
-        nc.vector.tensor_reduce(neg_max_b[:], bm[:], AX.X, ALU.max, negate=True)
-        p_b = sb.tile([P, 2, P, 2], F32, name="p_b", align_bytes=64)
-        sum_b = sb.tile([P, 1], F32, name="sum_b")
-        nc.scalar.activation(
-            p_b[:], bm[:].rearrange("q (p u e) -> q u p e", u=2, e=2), ACT.Exp, bias=neg_max_b[:], accum_out=sum_b[:]
+            nc.vector.tensor_tensor(bm[:, cols], b_ps[h], mask_sb[:, cols], ALU.add)
+        neg_b = sb.tile([P, 2, P, 2], F32, name="neg_b", align_bytes=64)
+        neg_max = sb.tile([P, 1], F32, name="neg_max")
+        nc.vector.tensor_scalar(
+            neg_b[:], bm[:].rearrange("q (p u e) -> q u p e", u=2, e=2), -1.0, neg_max_a[:], ALU.mult, ALU.min,
+            accum_out=neg_max[:],
         )
 
-        neg_a = sb.tile([P, 2, P, 2], F32, name="neg_a", align_bytes=64)
-        key_words = [sb.tile([P, HALF], U32, name="key_words%d" % h, align_bytes=64) for h in range(2)]
-        a_ps = [ps.tile([P, HALF], F32, name="a_ps%d" % h, tag="bank%d" % (2 + h)) for h in range(2)]
-        for h in range(2):
-            nc.vector.tensor_copy(
-                key_words[h][:], pool_words[:].bitcast(U32).indirect(offsets[:, 16 * h : 16 * (h + 1)])
-            )
-            product(
-                a_ps[h][:], q_op[2][:], q_op[3][:], key_words[h][:], key_scales[:, h * HALF : (h + 1) * HALF], True, True
-            )
-        neg_max = neg_max_b
-        for h in range(2):
-            lower = sb.tile([P, 1], F32, name="neg_max%d" % h)
-            nc.vector.tensor_scalar(
-                neg_a[:, :, 64 * h : 64 * (h + 1), :],
-                a_ps[h][:].rearrange("q (p u e) -> q u p e", u=2, e=2),
-                -1.0,
-                neg_max[:],
-                ALU.mult,
-                ALU.min,
-                accum_out=lower[:],
-            )
-            neg_max = lower
-
-        fac_ps = [ps.tile([P, 4, P], F32, name="fac_ps%d" % g, tag="bank%d" % (4 + g)) for g in range(2)]
-        for g in range(2):
-            for t in range(4):
-                nc.tensor.transpose(fac_ps[g][:, t, :], fac_cols[:, g, t : t + 1].to_broadcast([P, P]), ident[:])
-
-        shift_b = sb.tile([P, 1], F32, name="shift_b")
-        nc.scalar.activation(shift_b[:], neg_max_b[:], ACT.Exp, bias=neg_max[:], scale=-1.0)
+        v_grouped = [grouped_tile("v0", HALF)]
+        for piece in range(2):
+            interleave(scalar_cast, v_grouped[0], v_raw[0], piece * PIECE, piece * PIECE, PIECE)
         p_a = sb.tile([P, 2, P, 2], F32, name="p_a", align_bytes=64)
         sum_a = sb.tile([P, 1], F32, name="sum_a")
-        nc.scalar.activation(p_a[:], neg_a[:], ACT.Exp, bias=neg_max[:], scale=-1.0, accum_out=sum_a[:])
+        nc.scalar.activation(p_a[:], neg_a[:], ACT.Exp, bias=neg_max_a[:], scale=-1.0, accum_out=sum_a[:])
+        pf_a = sb.tile([P, 2, P, 2], F32, name="pf_a", align_bytes=64)
+        nc.gpsimd.tensor_tensor(pf_a[:], p_a[:], fac_a[:], ALU.mult)
 
-        def fac_view(g, u):
-            return fac_ps[g][:, 2 * u : 2 * u + 2, :].rearrange("q e p -> q p e")
+        v_grouped.append(grouped_tile("v1", HALF, tag="mask_sb"))
+        interleave(scalar_cast, v_grouped[1], v_raw[1], 0, 0, PIECE)
+        shift_a = sb.tile([P, 1], F32, name="shift_a")
+        nc.scalar.activation(shift_a[:], neg_max_a[:], ACT.Exp, bias=neg_max[:], scale=-1.0)
+        p_b = sb.tile([P, 2, P, 2], F32, name="p_b", tag="p_b", align_bytes=64)
+        sum_b = sb.tile([P, 1], F32, name="sum_b", tag="sum_b", align_bytes=64)
+        nc.scalar.activation(p_b[:], neg_b[:], ACT.Exp, bias=neg_max[:], scale=-1.0, accum_out=sum_b[:])
 
-        pf_b = sb.tile([P, 2, P, 2], F32, name="pf_b", align_bytes=64)
-        for u in range(2):
-            nc.vector.scalar_tensor_tensor(pf_b[:, u], p_b[:, u], shift_b[:], fac_view(1, u), ALU.mult, ALU.mult)
+        v_mx = [quantize("v0", v_grouped[0], tag="bm")]
+        interleave(nc.vector.tensor_copy, v_grouped[1], v_raw[1], PIECE, PIECE, PIECE)
         total = sb.tile([P, 1], F32, name="total")
-        nc.vector.tensor_scalar(total[:], sum_b[:], shift_b[:], sum_a[:], ALU.mult, ALU.add)
+        nc.vector.tensor_scalar(total[:], sum_a[:], shift_a[:], sum_b[:], ALU.mult, ALU.add)
         inv = sb.tile([P, 1], F32, name="inv")
         nc.vector.reciprocal(inv[:], total[:])
+        v_mx.append(quantize("v1", v_grouped[1], tag="sum_b"))
+        v_grouped.append(grouped_tile("v2", HALF))
+        interleave(scalar_cast, v_grouped[2], v_raw[2], 0, 0, PIECE)
+        interleave(nc.vector.tensor_copy, v_grouped[2], v_raw[2], PIECE, PIECE, PIECE)
 
         w = {(g, u): sb.tile([P, P, 2], BF16, name="w%d%d" % (g, u), align_bytes=64) for g in range(2) for u in range(2)}
-        for u in range(2):
-            nc.vector.scalar_tensor_tensor(w[0, u][:], p_a[:, u], inv[:], fac_view(0, u), ALU.mult, ALU.mult)
-            nc.scalar.activation(w[1, u][:], pf_b[:, u], ACT.Copy, scale=inv[:])
+        inv_a = sb.tile([P, 1], F32, name="inv_a")
 
-        wt_ps = [ps.tile([P, 2, P], F32, name="wt_ps%d" % g, tag="bank%d" % (6 + g)) for g in range(2)]
+        def draft_weights(u):
+            fac_b = draft_banks[u][:, 0:2, :].rearrange("q e p -> q p e")
+            nc.vector.scalar_tensor_tensor(w[1, u][:], p_b[:, u], inv[:], fac_b, ALU.mult, ALU.mult)
+
+        draft_weights(0)
+        nc.vector.tensor_tensor(inv_a[:], inv[:], shift_a[:], ALU.mult)
+        draft_weights(1)
         for u in range(2):
-            for g in range(2):
+            nc.scalar.activation(w[0, u][:], pf_a[:, u], ACT.Copy, scale=inv_a[:])
+
+        wt_ps = [ps.tile([P, 2, P], F32, name="wt_ps%d" % g) for g in range(2)]
+        for u in range(2):
+            for g in (1, 0):
                 nc.tensor.transpose(
                     wt_ps[g][:, u, :], w[g, u][:].rearrange("q p e -> q (p e)").bitcast(F32), ident[:]
                 )
-        w_codes, w_scales = [], []
-        for g in range(2):
-            grouped = sb.tile([P, Q, 4], BF16, name="wt_grouped%d" % g, align_bytes=64)
-            w_codes.append(sb.tile([P, Q], U32, name="wt_codes%d" % g, align_bytes=64))
-            w_scales.append(sb.tile([P, Q], U8, name="wt_scales%d" % g, align_bytes=64))
-            copy = nc.vector.tensor_copy if g == 0 else nc.scalar.copy
+        v_grouped.append(grouped_tile("v3", HALF))
+        interleave(scalar_cast, v_grouped[3], v_raw[3], 0, 0, PIECE)
+        interleave(nc.vector.tensor_copy, v_grouped[3], v_raw[3], PIECE, PIECE, PIECE)
+        v_mx.append(quantize("v2", v_grouped[2], tag="p_b"))
+        wt_grouped = [grouped_tile("wt%d" % g, Q) for g in range(2)]
+        for g, copy in ((1, nc.vector.tensor_copy), (0, nc.scalar.copy)):
             copy(
-                grouped[:].rearrange("p q t -> p (q t)").bitcast(F32).rearrange("p (q u) -> p q u", u=2),
+                wt_grouped[g][:].rearrange("p q t -> p (q t)").bitcast(F32).rearrange("p (q u) -> p q u", u=2),
                 wt_ps[g][:].rearrange("p u q -> p q u"),
             )
-            quantize(w_codes[g], w_scales[g], grouped)
+        v_mx.append(quantize("v3", v_grouped[3]))
+        w_mx = {g: quantize("wt%d" % g, wt_grouped[g]) for g in (1, 0)}
 
-        for n, gh in enumerate(v_order):
-            raw, grouped, codes, scales = v_op[gh]
-            interleave(nc.scalar.copy, grouped, raw, 0, PIECE)
-            interleave(nc.vector.tensor_copy if n >= 2 else nc.scalar.copy, grouped, raw, PIECE, PIECE)
-            quantize(codes, scales, grouped)
-
+        acc = [ps.tile([P, HALF], F32, name="o_ps%d" % h) for h in range(2)]
+        for g in (1, 0):
+            for h in range(2):
+                codes, scales = v_mx[2 * (1 - g) + h]
+                product(acc[h][:], w_mx[g][0][:], w_mx[g][1][:], codes[:], scales[:], g == 1, g == 0)
         for h in range(2):
-            acc = ps.tile([P, HALF], F32, name="o_ps%d" % h, tag="bank%d" % h)
-            for g in (1, 0):
-                product(acc[:], w_codes[g][:], w_scales[g][:], v_op[g, h][2][:], v_op[g, h][3][:], g == 1, g == 0)
             result = sb.tile([P, HALF], F32, name="result%d" % h, align_bytes=64)
             if h == 0:
-                nc.scalar.copy(result[:], acc[:])
+                nc.vector.tensor_copy(result[:], acc[h][:])
+                nc.sync.dma_start(out[:, h * HALF : (h + 1) * HALF], result[:])
             else:
-                nc.vector.tensor_copy(result[:], acc[:])
-            nc.sync.dma_start(out[:, h * HALF : (h + 1) * HALF], result[:])
+                nc.scalar.copy(result[:], acc[h][:])
+                nc.scalar.dma_start(out[:, h * HALF : (h + 1) * HALF], result[:])

@@ -147,10 +147,10 @@ def tile_attend_treeverify_kernel(tc, query, keys_words, keys_scales, dkey, mask
         for piece in range(2):
             interleave(scalar_cast, v_grouped[0], v_raw[0], piece * PIECE, piece * PIECE, PIECE)
         p_a = sb.tile([P, 2, P, 2], F32, name="p_a", align_bytes=64)
-        sum_a = sb.tile([P, 1], F32, name="sum_a")
+        sum_a = sb.tile([P, 1], F32, name="sum_a", tag="sum_a", align_bytes=64)
         nc.scalar.activation(p_a[:], neg_a[:], ACT.Exp, bias=neg_max_a[:], scale=-1.0, accum_out=sum_a[:])
-        pf_a = sb.tile([P, 2, P, 2], F32, name="pf_a", align_bytes=64)
-        nc.gpsimd.tensor_tensor(pf_a[:], p_a[:], fac_a[:], ALU.mult)
+        pf_a = [sb.tile([P, P, 2], F32, name="pf_a0", align_bytes=64)]
+        nc.gpsimd.tensor_tensor(pf_a[0][:], p_a[:, 0], fac_a[:, 0], ALU.mult)
 
         v_grouped.append(grouped_tile("v1", HALF, tag="mask_sb"))
         interleave(scalar_cast, v_grouped[1], v_raw[1], 0, 0, PIECE)
@@ -164,6 +164,8 @@ def tile_attend_treeverify_kernel(tc, query, keys_words, keys_scales, dkey, mask
         interleave(nc.vector.tensor_copy, v_grouped[1], v_raw[1], PIECE, PIECE, PIECE)
         total = sb.tile([P, 1], F32, name="total")
         nc.vector.tensor_scalar(total[:], sum_a[:], shift_a[:], sum_b[:], ALU.mult, ALU.add)
+        pf_a.append(sb.tile([P, P, 2], F32, name="pf_a1", tag="sum_a", align_bytes=64))
+        nc.gpsimd.tensor_tensor(pf_a[1][:], p_a[:, 1], fac_a[:, 1], ALU.mult)
         inv = sb.tile([P, 1], F32, name="inv")
         nc.vector.reciprocal(inv[:], total[:])
         v_mx.append(quantize("v1", v_grouped[1], tag="sum_b"))
@@ -178,11 +180,11 @@ def tile_attend_treeverify_kernel(tc, query, keys_words, keys_scales, dkey, mask
             fac_b = draft_banks[u][:, 0:2, :].rearrange("q e p -> q p e")
             nc.vector.scalar_tensor_tensor(w[1, u][:], p_b[:, u], inv[:], fac_b, ALU.mult, ALU.mult)
 
+        nc.scalar.activation(inv_a[:], inv[:], ACT.Copy, scale=shift_a[:])
         draft_weights(0)
-        nc.vector.tensor_tensor(inv_a[:], inv[:], shift_a[:], ALU.mult)
         draft_weights(1)
         for u in range(2):
-            nc.scalar.activation(w[0, u][:], pf_a[:, u], ACT.Copy, scale=inv_a[:])
+            nc.scalar.activation(w[0, u][:], pf_a[u][:], ACT.Copy, scale=inv_a[:])
 
         wt_ps = [ps.tile([P, 2, P], F32, name="wt_ps%d" % g) for g in range(2)]
         for u in range(2):
@@ -190,7 +192,7 @@ def tile_attend_treeverify_kernel(tc, query, keys_words, keys_scales, dkey, mask
                 nc.tensor.transpose(
                     wt_ps[g][:, u, :], w[g, u][:].rearrange("q p e -> q (p e)").bitcast(F32), ident[:]
                 )
-        v_grouped.append(grouped_tile("v3", HALF))
+        v_grouped.append(grouped_tile("v3", HALF, tag="sum_a"))
         interleave(scalar_cast, v_grouped[3], v_raw[3], 0, 0, PIECE)
         interleave(nc.vector.tensor_copy, v_grouped[3], v_raw[3], PIECE, PIECE, PIECE)
         v_mx.append(quantize("v2", v_grouped[2], tag="p_b"))
@@ -200,8 +202,8 @@ def tile_attend_treeverify_kernel(tc, query, keys_words, keys_scales, dkey, mask
                 wt_grouped[g][:].rearrange("p q t -> p (q t)").bitcast(F32).rearrange("p (q u) -> p q u", u=2),
                 wt_ps[g][:].rearrange("p u q -> p q u"),
             )
-        v_mx.append(quantize("v3", v_grouped[3]))
         w_mx = {g: quantize("wt%d" % g, wt_grouped[g]) for g in (1, 0)}
+        v_mx.append(quantize("v3", v_grouped[3]))
 
         acc = [ps.tile([P, HALF], F32, name="o_ps%d" % h) for h in range(2)]
         for g in (1, 0):

from contextlib import ExitStack

import concourse.mybir as mybir
from concourse.masks import make_identity

D, T, I, Q, E, J, C = 512, 2048, 512, 128, 512, 512, 1024
FLOPS = 2 * Q * D * (I + J) + 2 * Q * C * E

F32 = mybir.dt.float32
BF16 = mybir.dt.bfloat16
I32 = mybir.dt.int32
U32 = mybir.dt.uint32
U16 = mybir.dt.uint16
U8 = mybir.dt.uint8
FP8X4 = mybir.dt.float8_e4m3fn_x4
ALU = mybir.AluOpType
ACT = mybir.ActivationFunctionType
AX = mybir.AxisListType

P = 128
HALF = 256
PIECE = 128
SCALAR_SHARE = 96


def interleave(copy, grouped, raw, g0, c0, width):
    copy(
        grouped[:, g0 : g0 + width, :].rearrange("p (c i) t -> p c t i", i=4),
        raw[:, :, c0 : c0 + width].rearrange("p t (c i) -> p c t i", i=4),
    )


def tile_attend_treeverify_kernel(tc, query, keys_words, keys_scales, dkey, mask, fac, vals, offs, out):
    nc = tc.nc
    with ExitStack() as ctx:
        sb = ctx.enter_context(tc.tile_pool(name="sb", bufs=1))
        ps = ctx.enter_context(tc.psum_pool(name="ps", bufs=1))

        def raw_tile(name, width):
            return sb.tile([P, 4, width], F32, name=name + "_raw", tag=name + "_raw", align_bytes=64)

        def grouped_tile(name, width, tag=None):
            return sb.tile([P, width, 4], BF16, name=name + "_grouped", tag=tag or name + "_grouped", align_bytes=64)

        def quantize(name, grouped, tag=None):
            width = grouped.shape[1]
            codes = sb.tile([P, width], U32, name=name + "_codes", tag=tag or name + "_codes", align_bytes=64)
            scales = sb.tile([P, width], U8, name=name + "_scales", align_bytes=64)
            nc.vector.quantize_mx(
                out=codes[:].bitcast(FP8X4), scales=scales[:], in_=grouped[:].rearrange("p w t -> p (w t)")
            )
            return codes, scales

        def product(acc, lhs_codes, lhs_scales, rhs_codes, rhs_scales, start, stop):
            nc.tensor.matmul_mx(
                out=acc,
                lhsT=lhs_codes.bitcast(FP8X4),
                lhsT_scale=lhs_scales,
                rhs=rhs_codes.bitcast(FP8X4),
                rhs_scale=rhs_scales,
                start=start,
                stop=stop,
            )

        offsets = sb.tile([P, I // 16], U16, name="offsets")
        pool_scales = sb.tile([P, T], U8, name="pool_scales", align_bytes=64)
        pool_words = sb.tile([P, T], I32, name="pool_words", align_bytes=64)
        mask_sb = sb.tile([P, J], F32, name="mask_sb", tag="mask_sb", align_bytes=64)
        fac_cols = sb.tile([P, 2, 4], F32, name="fac_cols", align_bytes=64)
        q_raw = raw_tile("q", Q)
        d_raw = raw_tile("d", J)
        v_raw = [raw_tile("v%d" % n, HALF) for n in range(4)]
        val_rows = vals.rearrange("(g p t) w -> g p t w", g=2, t=4)

        def load_values(n):
            nc.sync.dma_start(v_raw[n][:], val_rows[1 - n // 2][:, :, (n % 2) * HALF : (n % 2 + 1) * HALF])

        nc.vector.memset(pool_scales[:].bitcast(I32), 0)
        nc.scalar.dma_start(fac_cols[:], fac.rearrange("o (g p t) -> p (o g) t", g=2, t=4))
        nc.sync.dma_start(offsets[:], offs)
        nc.sync.dma_start(pool_words[:], keys_words[0].rearrange("p n t -> p (n t)").bitcast(I32))
        for r in range(4):
            nc.sync.dma_start(pool_scales[r:P:32, :].bitcast(I32), keys_scales[0, r:16:4, :].bitcast(I32))
        nc.sync.dma_start(q_raw[:], query.rearrange("(p t) w -> p t w", t=4))
        nc.sync.dma_start(d_raw[:], dkey.rearrange("(p t) w -> p t w", t=4))
        load_values(0)
        nc.sync.dma_start(mask_sb[:], mask)
        for n in range(1, 4):
            load_values(n)

        ident = sb.tile([P, P], F32, name="ident", align_bytes=64)
        make_identity(nc, ident[:])

        def spread(out_ap, g, t):
            nc.tensor.transpose(out_ap, fac_cols[:, g, t : t + 1].to_broadcast([P, P]), ident[:])

        fac_a_ps = ps.tile([P, 4, P], F32, name="fac_a_ps", tag="prefix_bank")
        draft_banks = [ps.tile([P, 4, P], F32, name="draft_bank%d" % h) for h in range(2)]
        for t in range(4):
            spread(fac_a_ps[:, t, :], 0, t)
        for t in range(4):
            spread(draft_banks[t // 2][:, t % 2, :], 1, t)

        def scalar_cast(out_ap, in_ap):
            nc.scalar.activation(out_ap, in_ap, ACT.Copy)

        fac_a = sb.tile([P, 2, P, 2], F32, name="fac_a", align_bytes=64)
        scalar_cast(fac_a[:], fac_a_ps[:].rearrange("q (u e) p -> q u p e", u=2))

        key_words = sb.tile([P, I], U32, name="key_words", align_bytes=64)
        nc.vector.tensor_copy(key_words[:], pool_words[:].bitcast(U32).indirect(offsets[:]))
        key_scales = sb.tile([P, I], U8, name="key_scales", align_bytes=64)
        nc.vector.tensor_copy(key_scales[:], pool_scales[:].indirect(offsets[:]))
        q_grouped = grouped_tile("q", Q)
        interleave(scalar_cast, q_grouped, q_raw, 0, 0, Q)
        q_codes, q_scales = quantize("q", q_grouped)
        a_ps = ps.tile([P, I], F32, name="a_ps", tag="prefix_bank")
        product(a_ps[:], q_codes[:], q_scales[:], key_words[:], key_scales[:], True, True)

        d_grouped = [grouped_tile("d%d" % h, HALF) for h in range(2)]
        for h in range(2):
            interleave(scalar_cast, d_grouped[h], d_raw, 0, h * HALF, SCALAR_SHARE)
            interleave(nc.vector.tensor_copy, d_grouped[h], d_raw, SCALAR_SHARE, h * HALF + SCALAR_SHARE, HALF - SCALAR_SHARE)
        b_ps = [bank[:, 2:4, :].rearrange("q a b -> q (a b)") for bank in draft_banks]
        for h in range(2):
            codes, scales = quantize("d%d" % h, d_grouped[h])
            product(b_ps[h], q_codes[:], q_scales[:], codes[:], scales[:], True, True)

        neg_a = sb.tile([P, 2, P, 2], F32, name="neg_a", tag="d0_grouped", align_bytes=64)
        neg_max_a = sb.tile([P, 1], F32, name="neg_max_a")
        nc.vector.tensor_scalar(
            neg_a[:], a_ps[:].rearrange("q (p u e) -> q u p e", u=2, e=2), -1.0, None, ALU.mult, ALU.min,
            accum_out=neg_max_a[:],
        )
        bm = sb.tile([P, J], F32, name="bm", tag="bm", align_bytes=64)
        for h in range(2):
            cols = slice(h * HALF, (h + 1) * HALF)
            nc.vector.tensor_tensor(bm[:, cols], b_ps[h], mask_sb[:, cols], ALU.add)
        neg_b = sb.tile([P, 2, P, 2], F32, name="neg_b", align_bytes=64)
        neg_max = sb.tile([P, 1], F32, name="neg_max")
        nc.vector.tensor_scalar(
            neg_b[:], bm[:].rearrange("q (p u e) -> q u p e", u=2, e=2), -1.0, neg_max_a[:], ALU.mult, ALU.min,
            accum_out=neg_max[:],
        )

        v_grouped = [grouped_tile("v0", HALF)]
        for piece in range(2):
            interleave(scalar_cast, v_grouped[0], v_raw[0], piece * PIECE, piece * PIECE, PIECE)
        p_a = sb.tile([P, 2, P, 2], F32, name="p_a", align_bytes=64)
        sum_a = sb.tile([P, 1], F32, name="sum_a", tag="sum_a", align_bytes=64)
        nc.scalar.activation(p_a[:], neg_a[:], ACT.Exp, bias=neg_max_a[:], scale=-1.0, accum_out=sum_a[:])
        pf_a = [sb.tile([P, P, 2], F32, name="pf_a0", align_bytes=64)]
        nc.gpsimd.tensor_tensor(pf_a[0][:], p_a[:, 0], fac_a[:, 0], ALU.mult)

        v_grouped.append(grouped_tile("v1", HALF, tag="mask_sb"))
        interleave(scalar_cast, v_grouped[1], v_raw[1], 0, 0, PIECE)
        shift_a = sb.tile([P, 1], F32, name="shift_a")
        nc.scalar.activation(shift_a[:], neg_max_a[:], ACT.Exp, bias=neg_max[:], scale=-1.0)
        p_b = sb.tile([P, 2, P, 2], F32, name="p_b", tag="p_b", align_bytes=64)
        sum_b = sb.tile([P, 1], F32, name="sum_b", tag="sum_b", align_bytes=64)
        nc.scalar.activation(p_b[:], neg_b[:], ACT.Exp, bias=neg_max[:], scale=-1.0, accum_out=sum_b[:])

        v_mx = [quantize("v0", v_grouped[0], tag="bm")]
        interleave(nc.vector.tensor_copy, v_grouped[1], v_raw[1], PIECE, PIECE, PIECE)
        total = sb.tile([P, 1], F32, name="total")
        nc.vector.tensor_scalar(total[:], sum_a[:], shift_a[:], sum_b[:], ALU.mult, ALU.add)
        pf_a.append(sb.tile([P, P, 2], F32, name="pf_a1", tag="sum_a", align_bytes=64))
        nc.gpsimd.tensor_tensor(pf_a[1][:], p_a[:, 1], fac_a[:, 1], ALU.mult)
        inv = sb.tile([P, 1], F32, name="inv")
        nc.vector.reciprocal(inv[:], total[:])
        v_mx.append(quantize("v1", v_grouped[1], tag="sum_b"))
        v_grouped.append(grouped_tile("v2", HALF))
        interleave(scalar_cast, v_grouped[2], v_raw[2], 0, 0, PIECE)
        interleave(nc.vector.tensor_copy, v_grouped[2], v_raw[2], PIECE, PIECE, PIECE)

        w = {(g, u): sb.tile([P, P, 2], BF16, name="w%d%d" % (g, u), align_bytes=64) for g in range(2) for u in range(2)}
        inv_a = sb.tile([P, 1], F32, name="inv_a")

        def draft_weights(u):
            fac_b = draft_banks[u][:, 0:2, :].rearrange("q e p -> q p e")
            nc.vector.scalar_tensor_tensor(w[1, u][:], p_b[:, u], inv[:], fac_b, ALU.mult, ALU.mult)

        nc.scalar.activation(inv_a[:], inv[:], ACT.Copy, scale=shift_a[:])
        draft_weights(0)
        draft_weights(1)
        for u in range(2):
            nc.scalar.activation(w[0, u][:], pf_a[u][:], ACT.Copy, scale=inv_a[:])

        wt_ps = [ps.tile([P, 2, P], F32, name="wt_ps%d" % g) for g in range(2)]
        for u in range(2):
            for g in (1, 0):
                nc.tensor.transpose(
                    wt_ps[g][:, u, :], w[g, u][:].rearrange("q p e -> q (p e)").bitcast(F32), ident[:]
                )
        v_grouped.append(grouped_tile("v3", HALF, tag="sum_a"))
        interleave(scalar_cast, v_grouped[3], v_raw[3], 0, 0, PIECE)
        interleave(nc.vector.tensor_copy, v_grouped[3], v_raw[3], PIECE, PIECE, PIECE)
        v_mx.append(quantize("v2", v_grouped[2], tag="p_b"))
        wt_grouped = [grouped_tile("wt%d" % g, Q) for g in range(2)]
        for g, copy in ((1, nc.vector.tensor_copy), (0, nc.scalar.copy)):
            copy(
                wt_grouped[g][:].rearrange("p q t -> p (q t)").bitcast(F32).rearrange("p (q u) -> p q u", u=2),
                wt_ps[g][:].rearrange("p u q -> p q u"),
            )
        w_mx = {g: quantize("wt%d" % g, wt_grouped[g]) for g in (1, 0)}
        v_mx.append(quantize("v3", v_grouped[3]))

        acc = [ps.tile([P, HALF], F32, name="o_ps%d" % h) for h in range(2)]
        for g in (1, 0):
            for h in range(2):
                codes, scales = v_mx[2 * (1 - g) + h]
                product(acc[h][:], w_mx[g][0][:], w_mx[g][1][:], codes[:], scales[:], g == 1, g == 0)
        for h in range(2):
            result = sb.tile([P, HALF], F32, name="result%d" % h, align_bytes=64)
            if h == 0:
                nc.vector.tensor_copy(result[:], acc[h][:])
                nc.sync.dma_start(out[:, h * HALF : (h + 1) * HALF], result[:])
            else:
                nc.scalar.copy(result[:], acc[h][:])
                nc.scalar.dma_start(out[:, h * HALF : (h + 1) * HALF], result[:])
